import numpy as np
import ml_dtypes


def mxq(x, axis, fmt="e4m3"):
    dtype, down = {"e4m3": (ml_dtypes.float8_e4m3fn, 7), "e5m2": (ml_dtypes.float8_e5m2, 14)}[fmt]
    v = np.moveaxis(np.asarray(x, np.float32).astype(ml_dtypes.bfloat16).astype(np.float64), axis, -1)
    blocks = v.reshape(v.shape[:-1] + (-1, 32))
    amax = np.abs(blocks).max(-1, keepdims=True)
    byte = np.maximum(np.where(amax > 0, np.frexp(amax)[1] - 1 + 127, 0) - down, 1)
    scale = np.exp2(byte - 127.0)
    codes = (blocks / scale).astype(np.float32).astype(dtype).astype(np.float64)
    return np.moveaxis((codes * scale).reshape(v.shape), -1, axis)


WIDE = False


def mx_kscale(k):
    if not WIDE:
        return np.ones(k)
    levels = np.array([24, -24, 12, -12, 0])
    if k % 512:
        return np.exp2(np.random.permutation(np.resize(levels, k // 32))).repeat(32)
    a = np.empty((k // 512, 16))
    for p in range(k // 512):
        a[p, :8] = np.random.permutation(np.resize(levels, 8))
        for g in range(8):
            far = levels[np.abs(levels - a[p, g]) >= 10]
            a[p, g + 8] = far[np.random.randint(len(far))]
    return np.exp2(a.ravel()).repeat(32)


def f64(x):
    return np.asarray(x).astype(np.float64)


def striped8(idx):
    return np.concatenate([v.reshape(-1, 16).T for v in idx]).astype(np.uint16)


def unstriped8(offs):
    return np.stack([offs[16 * g:16 * g + 16].T.reshape(-1) for g in range(8)]).astype(np.int64)


E2M1 = np.array([0.0, 0.5, 1.0, 1.5, 2.0, 3.0, 4.0, 6.0, -0.0, -0.5, -1.0, -1.5, -2.0, -3.0, -4.0, -6.0])


def pack_weight(w, fmt):
    k, n = w.shape
    w = f64(np.asarray(w, np.float32).astype(ml_dtypes.bfloat16)).reshape(k // 32, 32, n)
    amax = np.abs(w).max(1)
    if fmt == "e4m3":
        byte = np.frexp(amax)[1] - 1 + 127 - 7
    else:
        mant, ex = np.frexp(amax / 6.0)
        byte = np.where(mant > 0.5, ex, ex - 1) + 127
    byte = np.clip(np.where(amax > 0, byte, 1), 1, 254)
    scaled = (w * np.exp2(127.0 - byte)[:, None, :]).reshape(k, n).astype(np.float32)
    by_word = np.ascontiguousarray(scaled.reshape(k // 512, 128, 4, n).transpose(0, 1, 3, 2))
    if fmt == "e4m3":
        words = by_word.astype(ml_dtypes.float8_e4m3fn).view(np.uint8)
    else:
        c = by_word.astype(ml_dtypes.float4_e2m1fn).view(np.uint8) & 0xF
        words = (c[..., 0::2] | (c[..., 1::2] << 4)).reshape(k // 512, 128, 2 * n)
    return np.ascontiguousarray(words), np.ascontiguousarray(byte.astype(np.uint8).reshape(k // 512, 16, n))


def unpack_weight(words, scales, fmt):
    g, _, n = scales.shape
    words = np.ascontiguousarray(words).reshape(g, 128, n, -1)
    if fmt == "e4m3":
        vals = words.view(ml_dtypes.float8_e4m3fn).astype(np.float64)
    else:
        nib = np.empty((g, 128, n, 4), np.uint8)
        nib[..., 0::2] = words & 0xF
        nib[..., 1::2] = words >> 4
        vals = E2M1[nib]
    vals = vals * np.repeat(np.exp2(scales.astype(np.float64) - 127.0), 8, axis=1)[..., None]
    return vals.transpose(0, 1, 3, 2).reshape(g * 512, n)


def silu(f):
    return f / (1.0 + np.exp(-np.maximum(f, -700.0)))


K, L, N, T, J = 512, 512, 512, 2048, 1024


def setup_inputs():
    n = np.random.standard_normal
    s = mx_kscale(K)[:, None]
    s2 = mx_kscale(L)[:, None]
    p_wb = pack_weight(n((L, N)) / np.sqrt(L) / s2, "e2m1")
    return {
        "xT": (n((K, T)) * s).astype(np.float32),
        "wgt": np.repeat(np.random.uniform(0.5, 2.0, (8, J)), 16, axis=0).astype(np.float32),
        "zT": (n((L, T)) * s2).astype(np.float32),
        "wgt2": np.repeat(np.random.uniform(0.5, 2.0, (8, J)), 16, axis=0).astype(np.float32),
        "wa": (n((K, N)) / np.sqrt(K) / s).astype(np.float32),
        "wb_words": p_wb[0],
        "wb_scales": p_wb[1],
        "b": (0.3 * n(N)).astype(np.float32),
        "offs": striped8(np.stack([np.random.permutation(T)[:J] for _ in range(8)])),
        "offs2": striped8(np.stack([np.random.permutation(T)[:J] for _ in range(8)])),
    }


def reference(xT, wgt, zT, wgt2, wa, wb_words, wb_scales, b, offs, offs2):
    idx = unstriped8(offs)
    idx2 = unstriped8(offs2)
    rows = np.arange(K)
    xg = f64(wgt)[rows // 4 % 128] * f64(xT)[rows[:, None], idx[rows % 512 // 64]]
    xT_ = mxq(xg, 0, "e4m3")
    rows = np.arange(L)
    xg = f64(wgt2)[rows // 4 % 128] * f64(zT)[rows[:, None], idx2[rows % 512 // 64]]
    zT_ = mxq(xg, 0, "e4m3")
    wa_ = mxq(f64(wa), 0, "e4m3")
    wb_ = unpack_weight(wb_words, wb_scales, "e2m1")
    ya = wa_.T @ xT_
    yb = wb_.T @ zT_
    return silu(silu(ya) * yb + f64(b)[:, None])

@@ -1,0 +1,188 @@
+from contextlib import ExitStack
+
+import concourse.mybir as mybir
+
+K, L, N, T, J = 512, 512, 512, 2048, 1024
+FLOPS = 2 * (K + L) * N * J
+
+F32 = mybir.dt.float32
+BF16 = mybir.dt.bfloat16
+I32 = mybir.dt.int32
+U32 = mybir.dt.uint32
+U16 = mybir.dt.uint16
+U8 = mybir.dt.uint8
+FP8X4 = mybir.dt.float8_e4m3fn_x4
+FP4X4 = mybir.dt.float4_e2m1fn_x4
+MULT = mybir.AluOpType.mult
+SILU = mybir.ActivationFunctionType.Silu
+
+P = 128
+PACK = 4
+BANK = 512
+TILES = N // P
+X_CHUNKS = (256, 256, 256, 256)
+Z_CHUNKS = (128, 256, 256, 256, 128)
+
+
+def spans(widths):
+    starts = [sum(widths[:c]) for c in range(len(widths))]
+    return [(s, s + w) for s, w in zip(starts, widths)]
+
+
+def weave(copy, woven, planes):
+    copy(
+        out=woven.rearrange("p (c i) t -> p c t i", i=4),
+        in_=planes.rearrange("p t (c i) -> p c t i", i=4),
+    )
+
+
+def tile_list_glu_silu_kernel(
+    tc, xT, wgt, zT, wgt2, wa, wb_words, wb_scales, b, offs, offs2, out
+):
+    nc = tc.nc
+    with ExitStack() as ctx:
+        keep = ctx.enter_context(tc.tile_pool(name="keep", bufs=1))
+        psum = ctx.enter_context(tc.psum_pool(name="psum", bufs=8))
+
+        def quantize(name, woven, width):
+            codes = keep.tile([P, width], U32, name=name + "_codes", align_bytes=64)
+            scales = keep.tile([P, width], U8, name=name + "_scales", align_bytes=64)
+            nc.vector.quantize_mx(
+                out=codes[:].bitcast(FP8X4), scales=scales[:], in_=woven[:].rearrange("p j t -> p (j t)")
+            )
+            return codes, scales
+
+        def gather(dst, plane, lists, weights, lo, hi):
+            nc.vector.tensor_tensor(dst, plane[:].indirect(lists[:, lo // 16 : hi // 16]), weights, MULT)
+
+        warm = keep.tile([P, 8], F32, name="warm")
+        nc.gpsimd.memset(warm[:, 0:4], 0.0)
+        nc.scalar.activation(warm[:, 4:8], warm[:, 0:4], SILU)
+
+        wb_plane = keep.tile([P, N], U8, name="wb_plane", align_bytes=64)
+        nc.gpsimd.memset(wb_plane[:].bitcast(I32), 0)
+
+        x_lists = keep.tile([P, J // 16], U16, name="x_lists")
+        z_lists = keep.tile([P, J // 16], U16, name="z_lists")
+        x_planes = [keep.tile([P, T], F32, name="x_plane%d" % t) for t in range(PACK)]
+        z_planes = [keep.tile([P, T], F32, name="z_plane%d" % t) for t in range(PACK)]
+        x_wgt = [keep.tile([P, J // 2], F32, name="x_wgt%d" % h) for h in range(2)]
+        z_wgt = keep.tile([P, J], F32, name="z_wgt")
+        wa_raw = keep.tile([P, PACK, N], F32, name="wa_raw")
+        wb_codes = keep.tile([P, 2 * N], U8, name="wb_codes", align_bytes=64)
+        bias = keep.tile([P, TILES], F32, name="bias")
+        x_rows = xT.rearrange("(p t) s -> t p s", t=PACK)
+        z_rows = zT.rearrange("(p t) s -> t p s", t=PACK)
+
+        nc.sync.dma_start(x_lists[:], offs)
+        nc.sync.dma_start(x_wgt[0][:], wgt[:, 0 : J // 2])
+        nc.sync.dma_start(x_planes[0][:], x_rows[0])
+        nc.sync.dma_start(x_wgt[1][:], wgt[:, J // 2 : J])
+        for t in range(1, PACK):
+            nc.sync.dma_start(x_planes[t][:], x_rows[t])
+        nc.sync.dma_start(wa_raw[:], wa.rearrange("(p t) n -> p t n", t=PACK))
+        nc.sync.dma_start(z_lists[:], offs2)
+        nc.sync.dma_start(z_wgt[:], wgt2)
+        for t in range(PACK):
+            nc.sync.dma_start(z_planes[t][:], z_rows[t])
+        nc.sync.dma_start(wb_codes[:].bitcast(I32), wb_words[0].bitcast(I32))
+        for q in range(4):
+            nc.sync.dma_start(
+                wb_plane[32 * q : 32 * q + 4, :].bitcast(I32), wb_scales[0, 4 * q : 4 * q + 4, :].bitcast(I32)
+            )
+        with nc.allow_non_contiguous_dma(reason="one bias value a partition and row tile"):
+            nc.sync.dma_start(bias[:], b.rearrange("(m p) -> p m", p=P))
+
+        xg = keep.tile([P, PACK, J], F32, name="xg")
+        for h in range(2):
+            gather(xg[:, 0, h * 512 : h * 512 + 512], x_planes[0], x_lists, x_wgt[h][:], h * 512, h * 512 + 512)
+        for t in range(1, PACK - 1):
+            for h in range(2):
+                gather(xg[:, t, h * 512 : h * 512 + 512], x_planes[t], x_lists, x_wgt[h][:], h * 512, h * 512 + 512)
+        x_woven = []
+        for c, (lo, hi) in enumerate(spans(X_CHUNKS)):
+            gather(xg[:, PACK - 1, lo:hi], x_planes[PACK - 1], x_lists, x_wgt[lo // 512][:, lo % 512 : lo % 512 + hi - lo], lo, hi)
+            woven = keep.tile([P, hi - lo, PACK], BF16, name="x_woven%d" % c, align_bytes=64)
+            weave(nc.scalar.copy, woven[:], xg[:, :, lo:hi])
+            x_woven.append(woven)
+
+        wa_woven = keep.tile([P, N, PACK], BF16, name="wa_woven", align_bytes=64)
+        weave(nc.vector.tensor_copy, wa_woven[:], wa_raw[:])
+        x_mx = [quantize("x0", x_woven[0], X_CHUNKS[0])]
+        wa_codes, wa_plane = quantize("wa", wa_woven, N)
+        gate = keep.tile([P, TILES, J], F32, name="gate")
+        for c, (lo, hi) in enumerate(spans(X_CHUNKS)):
+            if c > 0:
+                x_mx.append(quantize("x%d" % c, x_woven[c], hi - lo))
+            codes, scales = x_mx[c]
+            width = hi - lo
+            per_bank = BANK // width
+            for m0 in range(0, TILES, per_bank):
+                bank = psum.tile([P, per_bank, width], F32, name="bank")
+                for m in range(m0, m0 + per_bank):
+                    cols = slice(m * P, (m + 1) * P)
+                    nc.tensor.matmul_mx(
+                        out=bank[:, m - m0, :],
+                        lhsT=wa_codes[:, cols].bitcast(FP8X4),
+                        lhsT_scale=wa_plane[:, cols],
+                        rhs=codes[:].bitcast(FP8X4),
+                        rhs_scale=scales[:],
+                        start=True,
+                        stop=True,
+                    )
+                nc.scalar.activation(gate[:, m0 : m0 + per_bank, lo:hi], bank[:], SILU)
+
+        zg = keep.tile([P, PACK, J], F32, name="zg")
+        for t in range(PACK - 1):
+            gather(zg[:, t, :], z_planes[t], z_lists, z_wgt[:], 0, J)
+        out_rows = out.rearrange("(m p) j -> p m j", p=P)
+        chunks = spans(Z_CHUNKS)
+        z_woven = {}
+        z_banks = {}
+
+        def pick(c):
+            lo, hi = chunks[c]
+            gather(zg[:, PACK - 1, lo:hi], z_planes[PACK - 1], z_lists, z_wgt[:, lo:hi], lo, hi)
+            woven = keep.tile([P, hi - lo, PACK], BF16, name="z_woven%d" % c, align_bytes=64)
+            weave(nc.scalar.copy, woven[:], zg[:, :, lo:hi])
+            return woven
+
+        def project(c, woven):
+            lo, hi = chunks[c]
+            width = hi - lo
+            codes, scales = quantize("z%d" % c, woven, width)
+            per_bank = min(BANK // width, TILES)
+            banks = []
+            for m0 in range(0, TILES, per_bank):
+                bank = psum.tile([P, per_bank, width], F32, name="bank")
+                for m in range(m0, m0 + per_bank):
+                    nc.tensor.matmul_mx(
+                        out=bank[:, m - m0, :],
+                        lhsT=wb_codes[:, 2 * m * P : 2 * (m + 1) * P].bitcast(FP4X4),
+                        lhsT_scale=wb_plane[:, m * P : (m + 1) * P],
+                        rhs=codes[:].bitcast(FP8X4),
+                        rhs_scale=scales[:],
+                        start=True,
+                        stop=True,
+                    )
+                banks.append((m0, per_bank, bank))
+            return banks
+
+        def finish(c, banks):
+            lo, hi = chunks[c]
+            for m0, count, bank in banks:
+                gated = keep.tile([P, count, hi - lo], F32, name="gated%d_%d" % (c, m0))
+                nc.vector.tensor_tensor(gated[:], bank[:], gate[:, m0 : m0 + count, lo:hi], MULT)
+                result = keep.tile([P, count, hi - lo], F32, name="result%d_%d" % (c, m0))
+                for m in range(m0, m0 + count):
+                    nc.scalar.activation(result[:, m - m0, :], gated[:, m - m0, :], SILU, bias=bias[:, m : m + 1])
+                nc.sync.dma_start(out_rows[:, m0 : m0 + count, lo:hi], result[:])
+
+        for step in range(len(chunks) + 2):
+            woven = None
+            if step < len(chunks):
+                z_woven.setdefault(step, pick(step))
+            if 0 <= step - 1 < len(chunks):
+                z_banks.setdefault(step - 1, project(step - 1, z_woven.get(step - 1)))
+            if 0 <= step - 2 < len(chunks):
+                finish(step - 2, z_banks.get(step - 2))

@@ -1,6 +1,7 @@
 from contextlib import ExitStack
 
 import concourse.mybir as mybir
+from concourse.masks import make_identity
 
 K, L, N, T, J = 512, 512, 512, 2048, 1024
 FLOPS = 2 * (K + L) * N * J
@@ -20,8 +21,9 @@ P = 128
 PACK = 4
 BANK = 512
 TILES = N // P
+GROUPS, GROUP = 8, 16
 X_CHUNKS = (256, 256, 256, 256)
-Z_CHUNKS = (128, 256, 256, 256, 128)
+Z_CHUNKS = (256, 256, 256, 256)
 
 
 def spans(widths):
@@ -55,10 +57,10 @@ def tile_list_glu_silu_kernel(
         def gather(dst, plane, lists, weights, lo, hi):
             nc.vector.tensor_tensor(dst, plane[:].indirect(lists[:, lo // 16 : hi // 16]), weights, MULT)
 
-        warm = keep.tile([P, 8], F32, name="warm")
-        nc.gpsimd.memset(warm[:, 0:4], 0.0)
-        nc.scalar.activation(warm[:, 4:8], warm[:, 0:4], SILU)
-
+        rows = keep.tile([P, J], F32, name="rows")
+        nc.vector.memset(rows[:], 0.0)
+        ident = keep.tile([P, P], F32, name="ident")
+        make_identity(nc, ident[:])
         wb_plane = keep.tile([P, N], U8, name="wb_plane", align_bytes=64)
         nc.gpsimd.memset(wb_plane[:].bitcast(I32), 0)
 
@@ -66,7 +68,7 @@ def tile_list_glu_silu_kernel(
         z_lists = keep.tile([P, J // 16], U16, name="z_lists")
         x_planes = [keep.tile([P, T], F32, name="x_plane%d" % t) for t in range(PACK)]
         z_planes = [keep.tile([P, T], F32, name="z_plane%d" % t) for t in range(PACK)]
-        x_wgt = [keep.tile([P, J // 2], F32, name="x_wgt%d" % h) for h in range(2)]
+        x_wgt = keep.tile([P, J], F32, name="x_wgt")
         z_wgt = keep.tile([P, J], F32, name="z_wgt")
         wa_raw = keep.tile([P, PACK, N], F32, name="wa_raw")
         wb_codes = keep.tile([P, 2 * N], U8, name="wb_codes", align_bytes=64)
@@ -75,14 +77,16 @@ def tile_list_glu_silu_kernel(
         z_rows = zT.rearrange("(p t) s -> t p s", t=PACK)
 
         nc.sync.dma_start(x_lists[:], offs)
-        nc.sync.dma_start(x_wgt[0][:], wgt[:, 0 : J // 2])
+        nc.sync.dma_start(x_wgt[:, 0 : J // 2], wgt[:, 0 : J // 2])
         nc.sync.dma_start(x_planes[0][:], x_rows[0])
-        nc.sync.dma_start(x_wgt[1][:], wgt[:, J // 2 : J])
-        for t in range(1, PACK):
+        nc.sync.dma_start(x_wgt[:, J // 2 : J], wgt[:, J // 2 : J])
+        nc.sync.dma_start(x_planes[1][:], x_rows[1])
+        nc.sync.dma_start(rows[0:P:GROUP, :], wgt2[0:P:GROUP, :])
+        nc.sync.dma_start(rows[1 : 1 + TILES, 0:P], b.rearrange("(m p) -> m p", p=P))
+        for t in range(2, PACK):
             nc.sync.dma_start(x_planes[t][:], x_rows[t])
         nc.sync.dma_start(wa_raw[:], wa.rearrange("(p t) n -> p t n", t=PACK))
         nc.sync.dma_start(z_lists[:], offs2)
-        nc.sync.dma_start(z_wgt[:], wgt2)
         for t in range(PACK):
             nc.sync.dma_start(z_planes[t][:], z_rows[t])
         nc.sync.dma_start(wb_codes[:].bitcast(I32), wb_words[0].bitcast(I32))
@@ -90,18 +94,30 @@ def tile_list_glu_silu_kernel(
             nc.sync.dma_start(
                 wb_plane[32 * q : 32 * q + 4, :].bitcast(I32), wb_scales[0, 4 * q : 4 * q + 4, :].bitcast(I32)
             )
-        with nc.allow_non_contiguous_dma(reason="one bias value a partition and row tile"):
-            nc.sync.dma_start(bias[:], b.rearrange("(m p) -> p m", p=P))
+
+        per = BANK // P
+        for h in range(J // BANK):
+            turned = psum.tile([P, per, P], F32, name="bank")
+            for c in range(per):
+                nc.tensor.transpose(turned[:, c, :], rows[:, h * BANK + c * P : h * BANK + (c + 1) * P], ident[:])
+            if h == 0:
+                nc.scalar.copy(out=bias[:], in_=turned[:, 0, 1 : 1 + TILES])
+            spread = keep.tile([P, per, GROUPS, GROUP], F32, name="spread%d" % h)
+            heads = turned[:].rearrange("p c (g r) -> p c g r", r=GROUP)[:, :, :, 0:1]
+            nc.scalar.copy(out=spread[:], in_=heads.to_broadcast([P, per, GROUPS, GROUP]))
+            back = psum.tile([P, per, P], F32, name="bank")
+            for c in range(per):
+                nc.tensor.transpose(back[:, c, :], spread[:, c, :, :].rearrange("p g r -> p (g r)"), ident[:])
+            nc.scalar.copy(out=z_wgt[:, h * BANK : (h + 1) * BANK], in_=back[:].rearrange("p c j -> p (c j)"))
 
         xg = keep.tile([P, PACK, J], F32, name="xg")
         for h in range(2):
-            gather(xg[:, 0, h * 512 : h * 512 + 512], x_planes[0], x_lists, x_wgt[h][:], h * 512, h * 512 + 512)
+            gather(xg[:, 0, h * 512 : h * 512 + 512], x_planes[0], x_lists, x_wgt[:, h * 512 : h * 512 + 512], h * 512, h * 512 + 512)
         for t in range(1, PACK - 1):
-            for h in range(2):
-                gather(xg[:, t, h * 512 : h * 512 + 512], x_planes[t], x_lists, x_wgt[h][:], h * 512, h * 512 + 512)
+            gather(xg[:, t, :], x_planes[t], x_lists, x_wgt[:], 0, J)
         x_woven = []
         for c, (lo, hi) in enumerate(spans(X_CHUNKS)):
-            gather(xg[:, PACK - 1, lo:hi], x_planes[PACK - 1], x_lists, x_wgt[lo // 512][:, lo % 512 : lo % 512 + hi - lo], lo, hi)
+            gather(xg[:, PACK - 1, lo:hi], x_planes[PACK - 1], x_lists, x_wgt[:, lo:hi], lo, hi)
             woven = keep.tile([P, hi - lo, PACK], BF16, name="x_woven%d" % c, align_bytes=64)
             weave(nc.scalar.copy, woven[:], xg[:, :, lo:hi])
             x_woven.append(woven)
@@ -144,7 +160,7 @@ def tile_list_glu_silu_kernel(
             lo, hi = chunks[c]
             gather(zg[:, PACK - 1, lo:hi], z_planes[PACK - 1], z_lists, z_wgt[:, lo:hi], lo, hi)
             woven = keep.tile([P, hi - lo, PACK], BF16, name="z_woven%d" % c, align_bytes=64)
-            weave(nc.scalar.copy, woven[:], zg[:, :, lo:hi])
+            weave(nc.vector.tensor_copy if c == 9 else nc.scalar.copy, woven[:], zg[:, :, lo:hi])
             return woven
 
         def project(c, woven):
@@ -176,7 +192,11 @@ def tile_list_glu_silu_kernel(
                 result = keep.tile([P, count, hi - lo], F32, name="result%d_%d" % (c, m0))
                 for m in range(m0, m0 + count):
                     nc.scalar.activation(result[:, m - m0, :], gated[:, m - m0, :], SILU, bias=bias[:, m : m + 1])
-                nc.sync.dma_start(out_rows[:, m0 : m0 + count, lo:hi], result[:])
+                if c == len(chunks) - 1 and m0 + count == TILES:
+                    for m in range(count):
+                        nc.sync.dma_start(out_rows[:, m0 + m, lo:hi], result[:, m, :])
+                else:
+                    nc.sync.dma_start(out_rows[:, m0 : m0 + count, lo:hi], result[:])
 
         for step in range(len(chunks) + 2):
             woven = None

@@ -46,8 +46,9 @@ def tile_list_glu_silu_kernel(
         keep = ctx.enter_context(tc.tile_pool(name="keep", bufs=1))
         psum = ctx.enter_context(tc.psum_pool(name="psum", bufs=8))
 
-        def quantize(name, woven, width):
-            codes = keep.tile([P, width], U32, name=name + "_codes", align_bytes=64)
+        def quantize(name, woven, width, codes=None):
+            if codes is None:
+                codes = keep.tile([P, width], U32, name=name + "_codes", align_bytes=64)
             scales = keep.tile([P, width], U8, name=name + "_scales", align_bytes=64)
             nc.vector.quantize_mx(
                 out=codes[:].bitcast(FP8X4), scales=scales[:], in_=woven[:].rearrange("p j t -> p (j t)")
@@ -61,13 +62,15 @@ def tile_list_glu_silu_kernel(
         nc.vector.memset(rows[:], 0.0)
         ident = keep.tile([P, P], F32, name="ident")
         make_identity(nc, ident[:])
+        warm = keep.tile([P, 8], F32, name="warm")
+        nc.scalar.activation(warm[:, 0:1], ident[:, 0:1], SILU)
         wb_plane = keep.tile([P, N], U8, name="wb_plane", align_bytes=64)
         nc.gpsimd.memset(wb_plane[:].bitcast(I32), 0)
 
         x_lists = keep.tile([P, J // 16], U16, name="x_lists")
         z_lists = keep.tile([P, J // 16], U16, name="z_lists")
         x_planes = [keep.tile([P, T], F32, name="x_plane%d" % t) for t in range(PACK)]
-        z_planes = [keep.tile([P, T], F32, name="z_plane%d" % t) for t in range(PACK)]
+        z_planes = [keep.tile([P, T], F32, name="z_plane%d" % t, align_bytes=64) for t in range(PACK)]
         x_wgt = keep.tile([P, J], F32, name="x_wgt")
         z_wgt = keep.tile([P, J], F32, name="z_wgt")
         wa_raw = keep.tile([P, PACK, N], F32, name="wa_raw")
@@ -121,24 +124,31 @@ def tile_list_glu_silu_kernel(
             woven = keep.tile([P, hi - lo, PACK], BF16, name="x_woven%d" % c, align_bytes=64)
             weave(nc.scalar.copy, woven[:], xg[:, :, lo:hi])
             x_woven.append(woven)
+            if c == 1:
+                wa_second = keep.tile([P, 256, PACK], BF16, name="wa_second", align_bytes=64)
+                weave(nc.scalar.copy, wa_second[:], wa_raw[:, :, 256:N])
+        wa_first = keep.tile([P, 256, PACK], BF16, name="wa_first", align_bytes=64)
+        weave(nc.vector.tensor_copy, wa_first[:], wa_raw[:, :, 0:256])
 
-        wa_woven = keep.tile([P, N, PACK], BF16, name="wa_woven", align_bytes=64)
-        weave(nc.vector.tensor_copy, wa_woven[:], wa_raw[:])
-        x_mx = [quantize("x0", x_woven[0], X_CHUNKS[0])]
-        wa_codes, wa_plane = quantize("wa", wa_woven, N)
+        x_mx = [quantize("x0", x_woven[0], 256)]
+        wa_mx = [quantize("wa0", wa_first, 256)]
+        x_mx.append(quantize("x1", x_woven[1], 256))
+        zg = keep.tile([P, PACK, J], F32, name="zg")
+        gather(zg[:, 0, :], z_planes[0], z_lists, z_wgt[:], 0, J)
+        late_codes = keep.tile([P, 3, 256], U32, name="z_plane0", align_bytes=64)
+        x_mx.append(quantize("x2", x_woven[2], 256, late_codes[:, 0, :]))
+        wa_mx.append(quantize("wa1", wa_second, 256, late_codes[:, 1, :]))
+        x_mx.append(quantize("x3", x_woven[3], 256, late_codes[:, 2, :]))
         gate = keep.tile([P, TILES, J], F32, name="gate")
-        for c, (lo, hi) in enumerate(spans(X_CHUNKS)):
-            if c > 0:
-                x_mx.append(quantize("x%d" % c, x_woven[c], hi - lo))
-            codes, scales = x_mx[c]
-            width = hi - lo
-            per_bank = BANK // width
-            for m0 in range(0, TILES, per_bank):
-                bank = psum.tile([P, per_bank, width], F32, name="bank")
-                for m in range(m0, m0 + per_bank):
+        for m0 in range(0, TILES, 2):
+            wa_codes, wa_plane = wa_mx[m0 // 2]
+            for c, (lo, hi) in enumerate(spans(X_CHUNKS)):
+                codes, scales = x_mx[c]
+                bank = psum.tile([P, 2, hi - lo], F32, name="bank")
+                for m in range(2):
                     cols = slice(m * P, (m + 1) * P)
                     nc.tensor.matmul_mx(
-                        out=bank[:, m - m0, :],
+                        out=bank[:, m, :],
                         lhsT=wa_codes[:, cols].bitcast(FP8X4),
                         lhsT_scale=wa_plane[:, cols],
                         rhs=codes[:].bitcast(FP8X4),
@@ -146,10 +156,9 @@ def tile_list_glu_silu_kernel(
                         start=True,
                         stop=True,
                     )
-                nc.scalar.activation(gate[:, m0 : m0 + per_bank, lo:hi], bank[:], SILU)
+                nc.scalar.activation(gate[:, m0 : m0 + 2, lo:hi], bank[:], SILU)
 
-        zg = keep.tile([P, PACK, J], F32, name="zg")
-        for t in range(PACK - 1):
+        for t in range(1, PACK - 1):
             gather(zg[:, t, :], z_planes[t], z_lists, z_wgt[:], 0, J)
         out_rows = out.rearrange("(m p) j -> p m j", p=P)
         chunks = spans(Z_CHUNKS)

from contextlib import ExitStack

import concourse.mybir as mybir
from concourse.masks import make_identity

K, L, N, T, J = 512, 512, 512, 2048, 1024
FLOPS = 2 * (K + L) * N * J

F32 = mybir.dt.float32
BF16 = mybir.dt.bfloat16
I32 = mybir.dt.int32
U32 = mybir.dt.uint32
U16 = mybir.dt.uint16
U8 = mybir.dt.uint8
FP8X4 = mybir.dt.float8_e4m3fn_x4
FP4X4 = mybir.dt.float4_e2m1fn_x4
MULT = mybir.AluOpType.mult
SILU = mybir.ActivationFunctionType.Silu

P = 128
PACK = 4
BANK = 512
TILES = N // P
GROUPS, GROUP = 8, 16
X_CHUNKS = (256, 256, 256, 256)
Z_CHUNKS = (256, 256, 256, 256)


def spans(widths):
    starts = [sum(widths[:c]) for c in range(len(widths))]
    return [(s, s + w) for s, w in zip(starts, widths)]


def weave(copy, woven, planes):
    copy(
        out=woven.rearrange("p (c i) t -> p c t i", i=4),
        in_=planes.rearrange("p t (c i) -> p c t i", i=4),
    )


def tile_list_glu_silu_kernel(
    tc, xT, wgt, zT, wgt2, wa, wb_words, wb_scales, b, offs, offs2, out
):
    nc = tc.nc
    with ExitStack() as ctx:
        keep = ctx.enter_context(tc.tile_pool(name="keep", bufs=1))
        psum = ctx.enter_context(tc.psum_pool(name="psum", bufs=8))

        def quantize(name, woven, width, codes=None):
            if codes is None:
                codes = keep.tile([P, width], U32, name=name + "_codes", align_bytes=64)
            scales = keep.tile([P, width], U8, name=name + "_scales", align_bytes=64)
            nc.vector.quantize_mx(
                out=codes[:].bitcast(FP8X4), scales=scales[:], in_=woven[:].rearrange("p j t -> p (j t)")
            )
            return codes, scales

        def gather(dst, plane, lists, weights, lo, hi):
            nc.vector.tensor_tensor(dst, plane[:].indirect(lists[:, lo // 16 : hi // 16]), weights, MULT)

        rows = keep.tile([P, J], F32, name="rows")
        nc.vector.memset(rows[:], 0.0)
        ident = keep.tile([P, P], F32, name="ident")
        make_identity(nc, ident[:])
        warm = keep.tile([P, 8], F32, name="warm")
        nc.scalar.activation(warm[:, 0:1], ident[:, 0:1], SILU)
        wb_plane = keep.tile([P, N], U8, name="wb_plane", align_bytes=64)
        nc.gpsimd.memset(wb_plane[:].bitcast(I32), 0)

        x_lists = keep.tile([P, J // 16], U16, name="x_lists")
        z_lists = keep.tile([P, J // 16], U16, name="z_lists")
        x_planes = [keep.tile([P, T], F32, name="x_plane%d" % t) for t in range(PACK)]
        z_planes = [keep.tile([P, T], F32, name="z_plane%d" % t, align_bytes=64) for t in range(PACK)]
        x_wgt = keep.tile([P, J], F32, name="x_wgt")
        z_wgt = keep.tile([P, J], F32, name="z_wgt")
        wa_raw = keep.tile([P, PACK, N], F32, name="wa_raw")
        wb_codes = keep.tile([P, 2 * N], U8, name="wb_codes", align_bytes=64)
        bias = keep.tile([P, TILES], F32, name="bias")
        x_rows = xT.rearrange("(p t) s -> t p s", t=PACK)
        z_rows = zT.rearrange("(p t) s -> t p s", t=PACK)

        nc.sync.dma_start(x_lists[:], offs)
        nc.sync.dma_start(x_wgt[:, 0 : J // 2], wgt[:, 0 : J // 2])
        nc.sync.dma_start(x_planes[0][:], x_rows[0])
        nc.sync.dma_start(x_wgt[:, J // 2 : J], wgt[:, J // 2 : J])
        nc.sync.dma_start(x_planes[1][:], x_rows[1])
        nc.sync.dma_start(rows[0:P:GROUP, :], wgt2[0:P:GROUP, :])
        nc.sync.dma_start(rows[1 : 1 + TILES, 0:P], b.rearrange("(m p) -> m p", p=P))
        for t in range(2, PACK):
            nc.sync.dma_start(x_planes[t][:], x_rows[t])
        nc.sync.dma_start(wa_raw[:], wa.rearrange("(p t) n -> p t n", t=PACK))
        nc.sync.dma_start(z_lists[:], offs2)
        for t in range(PACK):
            nc.sync.dma_start(z_planes[t][:], z_rows[t])
        nc.sync.dma_start(wb_codes[:].bitcast(I32), wb_words[0].bitcast(I32))
        for q in range(4):
            nc.sync.dma_start(
                wb_plane[32 * q : 32 * q + 4, :].bitcast(I32), wb_scales[0, 4 * q : 4 * q + 4, :].bitcast(I32)
            )

        per = BANK // P
        for h in range(J // BANK):
            turned = psum.tile([P, per, P], F32, name="bank")
            for c in range(per):
                nc.tensor.transpose(turned[:, c, :], rows[:, h * BANK + c * P : h * BANK + (c + 1) * P], ident[:])
            if h == 0:
                nc.scalar.copy(out=bias[:], in_=turned[:, 0, 1 : 1 + TILES])
            spread = keep.tile([P, per, GROUPS, GROUP], F32, name="spread%d" % h)
            heads = turned[:].rearrange("p c (g r) -> p c g r", r=GROUP)[:, :, :, 0:1]
            nc.scalar.copy(out=spread[:], in_=heads.to_broadcast([P, per, GROUPS, GROUP]))
            back = psum.tile([P, per, P], F32, name="bank")
            for c in range(per):
                nc.tensor.transpose(back[:, c, :], spread[:, c, :, :].rearrange("p g r -> p (g r)"), ident[:])
            nc.scalar.copy(out=z_wgt[:, h * BANK : (h + 1) * BANK], in_=back[:].rearrange("p c j -> p (c j)"))

        xg = keep.tile([P, PACK, J], F32, name="xg")
        for h in range(2):
            gather(xg[:, 0, h * 512 : h * 512 + 512], x_planes[0], x_lists, x_wgt[:, h * 512 : h * 512 + 512], h * 512, h * 512 + 512)
        for t in range(1, PACK - 1):
            gather(xg[:, t, :], x_planes[t], x_lists, x_wgt[:], 0, J)
        x_woven = []
        for c, (lo, hi) in enumerate(spans(X_CHUNKS)):
            gather(xg[:, PACK - 1, lo:hi], x_planes[PACK - 1], x_lists, x_wgt[:, lo:hi], lo, hi)
            woven = keep.tile([P, hi - lo, PACK], BF16, name="x_woven%d" % c, align_bytes=64)
            weave(nc.scalar.copy, woven[:], xg[:, :, lo:hi])
            x_woven.append(woven)
            if c == 1:
                wa_second = keep.tile([P, 256, PACK], BF16, name="wa_second", align_bytes=64)
                weave(nc.scalar.copy, wa_second[:], wa_raw[:, :, 256:N])
        wa_first = keep.tile([P, 256, PACK], BF16, name="wa_first", align_bytes=64)
        weave(nc.vector.tensor_copy, wa_first[:], wa_raw[:, :, 0:256])

        x_mx = [quantize("x0", x_woven[0], 256)]
        wa_mx = [quantize("wa0", wa_first, 256)]
        x_mx.append(quantize("x1", x_woven[1], 256))
        zg = keep.tile([P, PACK, J], F32, name="zg")
        gather(zg[:, 0, :], z_planes[0], z_lists, z_wgt[:], 0, J)
        late_codes = keep.tile([P, 3, 256], U32, name="z_plane0", align_bytes=64)
        x_mx.append(quantize("x2", x_woven[2], 256, late_codes[:, 0, :]))
        wa_mx.append(quantize("wa1", wa_second, 256, late_codes[:, 1, :]))
        x_mx.append(quantize("x3", x_woven[3], 256, late_codes[:, 2, :]))
        gate = keep.tile([P, TILES, J], F32, name="gate")
        for m0 in range(0, TILES, 2):
            wa_codes, wa_plane = wa_mx[m0 // 2]
            for c, (lo, hi) in enumerate(spans(X_CHUNKS)):
                codes, scales = x_mx[c]
                bank = psum.tile([P, 2, hi - lo], F32, name="bank")
                for m in range(2):
                    cols = slice(m * P, (m + 1) * P)
                    nc.tensor.matmul_mx(
                        out=bank[:, m, :],
                        lhsT=wa_codes[:, cols].bitcast(FP8X4),
                        lhsT_scale=wa_plane[:, cols],
                        rhs=codes[:].bitcast(FP8X4),
                        rhs_scale=scales[:],
                        start=True,
                        stop=True,
                    )
                nc.scalar.activation(gate[:, m0 : m0 + 2, lo:hi], bank[:], SILU)

        for t in range(1, PACK - 1):
            gather(zg[:, t, :], z_planes[t], z_lists, z_wgt[:], 0, J)
        out_rows = out.rearrange("(m p) j -> p m j", p=P)
        chunks = spans(Z_CHUNKS)
        z_woven = {}
        z_banks = {}

        def pick(c):
            lo, hi = chunks[c]
            gather(zg[:, PACK - 1, lo:hi], z_planes[PACK - 1], z_lists, z_wgt[:, lo:hi], lo, hi)
            woven = keep.tile([P, hi - lo, PACK], BF16, name="z_woven%d" % c, align_bytes=64)
            weave(nc.vector.tensor_copy if c == 9 else nc.scalar.copy, woven[:], zg[:, :, lo:hi])
            return woven

        def project(c, woven):
            lo, hi = chunks[c]
            width = hi - lo
            codes, scales = quantize("z%d" % c, woven, width)
            per_bank = min(BANK // width, TILES)
            banks = []
            for m0 in range(0, TILES, per_bank):
                bank = psum.tile([P, per_bank, width], F32, name="bank")
                for m in range(m0, m0 + per_bank):
                    nc.tensor.matmul_mx(
                        out=bank[:, m - m0, :],
                        lhsT=wb_codes[:, 2 * m * P : 2 * (m + 1) * P].bitcast(FP4X4),
                        lhsT_scale=wb_plane[:, m * P : (m + 1) * P],
                        rhs=codes[:].bitcast(FP8X4),
                        rhs_scale=scales[:],
                        start=True,
                        stop=True,
                    )
                banks.append((m0, per_bank, bank))
            return banks

        def finish(c, banks):
            lo, hi = chunks[c]
            for m0, count, bank in banks:
                gated = keep.tile([P, count, hi - lo], F32, name="gated%d_%d" % (c, m0))
                nc.vector.tensor_tensor(gated[:], bank[:], gate[:, m0 : m0 + count, lo:hi], MULT)
                result = keep.tile([P, count, hi - lo], F32, name="result%d_%d" % (c, m0))
                for m in range(m0, m0 + count):
                    nc.scalar.activation(result[:, m - m0, :], gated[:, m - m0, :], SILU, bias=bias[:, m : m + 1])
                if c == len(chunks) - 1 and m0 + count == TILES:
                    for m in range(count):
                        nc.sync.dma_start(out_rows[:, m0 + m, lo:hi], result[:, m, :])
                else:
                    nc.sync.dma_start(out_rows[:, m0 : m0 + count, lo:hi], result[:])

        for step in range(len(chunks) + 2):
            woven = None
            if step < len(chunks):
                z_woven.setdefault(step, pick(step))
            if 0 <= step - 1 < len(chunks):
                z_banks.setdefault(step - 1, project(step - 1, z_woven.get(step - 1)))
            if 0 <= step - 2 < len(chunks):
                finish(step - 2, z_banks.get(step - 2))
